import numpy as np
import ml_dtypes


def mxq(x, axis, fmt="e4m3"):
    dtype, down = {"e4m3": (ml_dtypes.float8_e4m3fn, 7), "e5m2": (ml_dtypes.float8_e5m2, 14)}[fmt]
    v = np.moveaxis(np.asarray(x, np.float32).astype(ml_dtypes.bfloat16).astype(np.float64), axis, -1)
    blocks = v.reshape(v.shape[:-1] + (-1, 32))
    amax = np.abs(blocks).max(-1, keepdims=True)
    byte = np.maximum(np.where(amax > 0, np.frexp(amax)[1] - 1 + 127, 0) - down, 1)
    scale = np.exp2(byte - 127.0)
    codes = (blocks / scale).astype(np.float32).astype(dtype).astype(np.float64)
    return np.moveaxis((codes * scale).reshape(v.shape), -1, axis)


WIDE = False


def mx_kscale(k):
    if not WIDE:
        return np.ones(k)
    levels = np.array([10, -10, 5, -5, 0])
    if k % 512:
        return np.exp2(np.random.permutation(np.resize(levels, k // 32))).repeat(32)
    a = np.empty((k // 512, 16))
    for p in range(k // 512):
        a[p, :8] = np.random.permutation(np.resize(levels, 8))
        for g in range(8):
            far = levels[np.abs(levels - a[p, g]) >= 10]
            a[p, g + 8] = far[np.random.randint(len(far))]
    return np.exp2(a.ravel()).repeat(32)


def f64(x):
    return np.asarray(x).astype(np.float64)


E2M1 = np.array([0.0, 0.5, 1.0, 1.5, 2.0, 3.0, 4.0, 6.0, -0.0, -0.5, -1.0, -1.5, -2.0, -3.0, -4.0, -6.0])


def pack_weight(w, fmt):
    k, n = w.shape
    w = f64(np.asarray(w, np.float32).astype(ml_dtypes.bfloat16)).reshape(k // 32, 32, n)
    amax = np.abs(w).max(1)
    if fmt == "e4m3":
        byte = np.frexp(amax)[1] - 1 + 127 - 7
    else:
        mant, ex = np.frexp(amax / 6.0)
        byte = np.where(mant > 0.5, ex, ex - 1) + 127
    byte = np.clip(np.where(amax > 0, byte, 1), 1, 254)
    scaled = (w * np.exp2(127.0 - byte)[:, None, :]).reshape(k, n).astype(np.float32)
    by_word = np.ascontiguousarray(scaled.reshape(k // 512, 128, 4, n).transpose(0, 1, 3, 2))
    if fmt == "e4m3":
        words = by_word.astype(ml_dtypes.float8_e4m3fn).view(np.uint8)
    else:
        c = by_word.astype(ml_dtypes.float4_e2m1fn).view(np.uint8) & 0xF
        words = (c[..., 0::2] | (c[..., 1::2] << 4)).reshape(k // 512, 128, 2 * n)
    return np.ascontiguousarray(words), np.ascontiguousarray(byte.astype(np.uint8).reshape(k // 512, 16, n))


def unpack_weight(words, scales, fmt):
    g, _, n = scales.shape
    words = np.ascontiguousarray(words).reshape(g, 128, n, -1)
    if fmt == "e4m3":
        vals = words.view(ml_dtypes.float8_e4m3fn).astype(np.float64)
    else:
        nib = np.empty((g, 128, n, 4), np.uint8)
        nib[..., 0::2] = words & 0xF
        nib[..., 1::2] = words >> 4
        vals = E2M1[nib]
    vals = vals * np.repeat(np.exp2(scales.astype(np.float64) - 127.0), 8, axis=1)[..., None]
    return vals.transpose(0, 1, 3, 2).reshape(g * 512, n)


def silu(v):
    return v / (1.0 + np.exp(-np.maximum(v, -700.0)))


K, M, T = 1024, 1536, 512


def setup_inputs():
    n = np.random.standard_normal
    s = mx_kscale(K)[:, None]
    x = n((K, T)) * s
    x4 = pack_weight(x, "e2m1")
    rest = x - unpack_weight(*x4, "e2m1")
    p_w4 = pack_weight(n((K, M)) / np.sqrt(K) / s, "e2m1")
    return {
        "x4_words": x4[0],
        "x4_scales": x4[1],
        "xr": (rest).astype(np.float32),
        "w4_words": p_w4[0],
        "w4_scales": p_w4[1],
        "b": (0.3 * n(1536)).astype(np.float32),
    }


def reference(x4_words, x4_scales, xr, w4_words, w4_scales, b):
    x4_ = unpack_weight(x4_words, x4_scales, "e2m1")
    xr_ = mxq(f64(xr), 0, "e4m3")
    w4_ = unpack_weight(w4_words, w4_scales, "e2m1")
    y = w4_.T @ x4_ + w4_.T @ xr_
    return silu(y + f64(b)[:, None])

@@ -1,0 +1,160 @@
+from contextlib import ExitStack
+
+import concourse.mybir as mybir
+
+K, M, T = 1024, 1536, 512
+FLOPS = 2 * 2 * K * M * T
+
+F32 = mybir.dt.float32
+BF16 = mybir.dt.bfloat16
+I32 = mybir.dt.int32
+U32 = mybir.dt.uint32
+U8 = mybir.dt.uint8
+FP8X4 = mybir.dt.float8_e4m3fn_x4
+FP4X4 = mybir.dt.float4_e2m1fn_x4
+SILU = mybir.ActivationFunctionType.Silu
+
+P = 128
+PACK = 4
+PASSES = 2
+TILES = M // P
+BANKS = 8
+EARLY = 8
+HALF = T // 2
+LAG = 3
+VECTOR_COLS = 160
+
+
+def tile_mix_xres_fm_silu_kernel(tc, x4_words, x4_scales, xr, w4_words, w4_scales, b, out):
+    nc = tc.nc
+    with ExitStack() as ctx:
+        keep = ctx.enter_context(tc.tile_pool(name="keep", bufs=1))
+        psum = ctx.enter_context(tc.psum_pool(name="psum", bufs=1))
+        ctx.enter_context(tc.manual_schedule())
+
+        x_words = keep.tile([P, PASSES, 2 * T], U8, align_bytes=256)
+        x_scales = keep.tile([P, PASSES, T], U8, align_bytes=256)
+        we_words = [keep.tile([P, EARLY * 2 * P], U8, align_bytes=256, name="we_words%d" % a) for a in range(PASSES)]
+        we_scales = keep.tile([P, PASSES, EARLY * P], U8, align_bytes=256)
+        wl_words = keep.tile([P, PASSES, (TILES - EARLY) * 2 * P], U8, align_bytes=256)
+        wl_scales = keep.tile([P, PASSES, (TILES - EARLY) * P], U8, align_bytes=256)
+        warm = keep.tile([P, 1], F32)
+        warm_out = keep.tile([P, 1], F32)
+        b_rows = keep.tile([P, 32], F32, align_bytes=64)
+        b_cols = keep.tile([P, 32], F32, align_bytes=64)
+
+        nc.vector.memset(x_scales[:].bitcast(I32), 0)
+        nc.vector.memset(we_scales[:].bitcast(I32), 0)
+        nc.vector.memset(b_rows[:], 0.0)
+        nc.vector.memset(warm[:], 0.0)
+        nc.vector.memset(wl_scales[:].bitcast(I32), 0)
+
+        xw = x4_words.bitcast(I32).rearrange("a p n -> p a n")
+        ww = w4_words.bitcast(I32)
+        xs = x4_scales.bitcast(I32).rearrange("a (q r) n -> r q a n", r=4)
+        ws = w4_scales.bitcast(I32).rearrange("a (q r) n -> r q a n", r=4)
+        e_words = EARLY * 2 * P // 4
+        e_scales = EARLY * P // 4
+
+        nc.gpsimd.dma_start(out=x_words[:].bitcast(I32), in_=xw)
+        for a in range(PASSES):
+            nc.gpsimd.dma_start(out=we_words[a][:].bitcast(I32), in_=ww[a, :, 0:e_words])
+        b_view = b.rearrange("(i q c) -> q i c", q=4, c=32)
+        for q in range(4):
+            nc.gpsimd.dma_start(out=b_rows[32 * q : 32 * q + TILES, :], in_=b_view[q])
+
+        for r in range(4):
+            nc.sync.dma_start(out=x_scales[:].bitcast(I32)[r:P:32], in_=xs[r])
+        for r in range(4):
+            nc.scalar.dma_start(out=we_scales[:].bitcast(I32)[r:P:32], in_=ws[r, :, :, 0:e_scales])
+        nc.scalar.activation(warm_out[:], warm[:], SILU)
+
+        xr_view = xr.rearrange("(a p j) t -> a p j t", p=P, j=PACK)
+        raw = [keep.tile([P, PACK, T], F32, name="raw%d" % a) for a in range(PASSES)]
+        nc.sync.dma_start(out=raw[0][:], in_=xr_view[0])
+        for h in range(2):
+            cols = slice(h * HALF, (h + 1) * HALF)
+            nc.sync.dma_start(out=raw[1][:, :, cols], in_=xr_view[1, :, :, cols])
+        nc.sync.dma_start(out=wl_words[:].bitcast(I32), in_=ww.rearrange("a p n -> p a n")[:, :, e_words:])
+        for r in range(4):
+            nc.sync.dma_start(out=wl_scales[:].bitcast(I32)[r:P:32], in_=ws[r, :, :, e_scales:])
+
+        grouped = [keep.tile([P, T, PACK], BF16, align_bytes=256, name="grouped%d" % a) for a in range(PASSES)]
+        codes = [keep.tile([P, T], U32, align_bytes=256, name="codes%d" % a) for a in range(PASSES)]
+        scales = [keep.tile([P, T], U8, align_bytes=256, name="scales%d" % a) for a in range(PASSES)]
+
+        def interleave(a, h):
+            c0 = h * HALF
+            c1 = c0 + VECTOR_COLS
+            c2 = c0 + HALF
+            nc.vector.tensor_copy(out=grouped[a][:, c0:c1, :], in_=raw[a][:, :, c0:c1].rearrange("p j t -> p t j"))
+            nc.scalar.copy(out=grouped[a][:, c1:c2, :], in_=raw[a][:, :, c1:c2].rearrange("p j t -> p t j"))
+
+        def quantize(a, h):
+            cols = slice(h * HALF, (h + 1) * HALF)
+            nc.vector.quantize_mx(
+                out=codes[a][:, cols].bitcast(FP8X4),
+                scales=scales[a][:, cols],
+                in_=grouped[a][:, cols, :].rearrange("p t j -> p (t j)"),
+            )
+
+        interleave(0, 0)
+        interleave(0, 1)
+        quantize(0, 0)
+        quantize(0, 1)
+        interleave(1, 0)
+        quantize(1, 0)
+        interleave(1, 1)
+        quantize(1, 1)
+        nc.vector.transpose(b_cols[:], b_rows[:])
+
+        banks = {}
+        done = {}
+
+        def mx_pass(kind, i, a):
+            if i not in banks:
+                banks[i] = psum.tile([P, T], F32, name="acc%d" % i, tag="bank%d" % (i % BANKS))
+                done[i] = 0
+            if i < EARLY:
+                lhsT = we_words[a][:, 2 * P * i : 2 * P * (i + 1)].bitcast(FP4X4)
+                lhsT_scale = we_scales[:, a, P * i : P * (i + 1)]
+            else:
+                j = i - EARLY
+                lhsT = wl_words[:, a, 2 * P * j : 2 * P * (j + 1)].bitcast(FP4X4)
+                lhsT_scale = wl_scales[:, a, P * j : P * (j + 1)]
+            if kind == "x4":
+                rhs = x_words[:, a, :].bitcast(FP4X4)
+                rhs_scale = x_scales[:, a, :]
+            else:
+                rhs = codes[a][:].bitcast(FP8X4)
+                rhs_scale = scales[a][:]
+            nc.tensor.matmul_mx(
+                out=banks[i][:], lhsT=lhsT, lhsT_scale=lhsT_scale, rhs=rhs, rhs_scale=rhs_scale,
+                start=done[i] == 0, stop=done[i] == 3,
+            )
+            done[i] += 1
+            if done[i] == 4:
+                finish(i)
+
+        def finish(i):
+            pieces = 2 if i == TILES - 1 else 1
+            width = T // pieces
+            for c in range(pieces):
+                cols = slice(c * width, (c + 1) * width)
+                res = keep.tile([P, width], F32, name="res%d_%d" % (i, c))
+                nc.scalar.activation(res[:], banks[i][:, cols], SILU, bias=b_cols[:, i : i + 1])
+                nc.sync.dma_start(out=out[P * i : P * (i + 1), cols], in_=res[:])
+
+        for a in range(PASSES):
+            for i in range(BANKS):
+                mx_pass("x4", i, a)
+        for i in range(LAG):
+            mx_pass("xr", i, 0)
+        for i in range(BANKS):
+            mx_pass("xr", i, 1)
+            if i + LAG < BANKS:
+                mx_pass("xr", i + LAG, 0)
+        for i in range(BANKS, TILES):
+            for kind in ("x4", "xr"):
+                for a in range(PASSES):
+                    mx_pass(kind, i, a)

@@ -32,9 +32,13 @@ def tile_mix_xres_fm_silu_kernel(tc, x4_words, x4_scales, xr, w4_words, w4_scale
         psum = ctx.enter_context(tc.psum_pool(name="psum", bufs=1))
         ctx.enter_context(tc.manual_schedule())
 
-        x_words = keep.tile([P, PASSES, 2 * T], U8, align_bytes=256)
+        x_words = [keep.tile([P, 2 * T], U8, align_bytes=256, name="x_words%d" % a) for a in range(PASSES)]
         x_scales = keep.tile([P, PASSES, T], U8, align_bytes=256)
-        we_words = [keep.tile([P, EARLY * 2 * P], U8, align_bytes=256, name="we_words%d" % a) for a in range(PASSES)]
+        half_early = EARLY // 2
+        we_words = [
+            [keep.tile([P, half_early * 2 * P], U8, align_bytes=256, name="we_words%d_%d" % (a, g)) for g in range(2)]
+            for a in range(PASSES)
+        ]
         we_scales = keep.tile([P, PASSES, EARLY * P], U8, align_bytes=256)
         wl_words = keep.tile([P, PASSES, (TILES - EARLY) * 2 * P], U8, align_bytes=256)
         wl_scales = keep.tile([P, PASSES, (TILES - EARLY) * P], U8, align_bytes=256)
@@ -56,9 +60,8 @@ def tile_mix_xres_fm_silu_kernel(tc, x4_words, x4_scales, xr, w4_words, w4_scale
         e_words = EARLY * 2 * P // 4
         e_scales = EARLY * P // 4
 
-        nc.gpsimd.dma_start(out=x_words[:].bitcast(I32), in_=xw)
-        for a in range(PASSES):
-            nc.gpsimd.dma_start(out=we_words[a][:].bitcast(I32), in_=ww[a, :, 0:e_words])
+        nc.sync.dma_start(out=x_words[0][:].bitcast(I32), in_=xw[:, 0])
+        nc.scalar.dma_start(out=we_words[0][0][:].bitcast(I32), in_=ww[0, :, 0 : e_words // 2])
         b_view = b.rearrange("(i q c) -> q i c", q=4, c=32)
         for q in range(4):
             nc.gpsimd.dma_start(out=b_rows[32 * q : 32 * q + TILES, :], in_=b_view[q])
@@ -66,7 +69,14 @@ def tile_mix_xres_fm_silu_kernel(tc, x4_words, x4_scales, xr, w4_words, w4_scale
         for r in range(4):
             nc.sync.dma_start(out=x_scales[:].bitcast(I32)[r:P:32], in_=xs[r])
         for r in range(4):
-            nc.scalar.dma_start(out=we_scales[:].bitcast(I32)[r:P:32], in_=ws[r, :, :, 0:e_scales])
+            queue = nc.scalar if r < 2 else nc.sync
+            queue.dma_start(out=we_scales[:].bitcast(I32)[r:P:32], in_=ws[r, :, :, 0:e_scales])
+        nc.sync.dma_start(out=we_words[0][1][:].bitcast(I32), in_=ww[0, :, e_words // 2 : e_words])
+        nc.sync.dma_start(out=x_words[1][:].bitcast(I32), in_=xw[:, 1])
+        for g in range(2):
+            nc.sync.dma_start(
+                out=we_words[1][g][:].bitcast(I32), in_=ww[1, :, g * e_words // 2 : (g + 1) * e_words // 2]
+            )
         nc.scalar.activation(warm_out[:], warm[:], SILU)
 
         xr_view = xr.rearrange("(a p j) t -> a p j t", p=P, j=PACK)
@@ -116,14 +126,15 @@ def tile_mix_xres_fm_silu_kernel(tc, x4_words, x4_scales, xr, w4_words, w4_scale
                 banks[i] = psum.tile([P, T], F32, name="acc%d" % i, tag="bank%d" % (i % BANKS))
                 done[i] = 0
             if i < EARLY:
-                lhsT = we_words[a][:, 2 * P * i : 2 * P * (i + 1)].bitcast(FP4X4)
+                g, k = divmod(i, half_early)
+                lhsT = we_words[a][g][:, 2 * P * k : 2 * P * (k + 1)].bitcast(FP4X4)
                 lhsT_scale = we_scales[:, a, P * i : P * (i + 1)]
             else:
                 j = i - EARLY
                 lhsT = wl_words[:, a, 2 * P * j : 2 * P * (j + 1)].bitcast(FP4X4)
                 lhsT_scale = wl_scales[:, a, P * j : P * (j + 1)]
             if kind == "x4":
-                rhs = x_words[:, a, :].bitcast(FP4X4)
+                rhs = x_words[a][:].bitcast(FP4X4)
                 rhs_scale = x_scales[:, a, :]
             else:
                 rhs = codes[a][:].bitcast(FP8X4)

@@ -22,6 +22,7 @@ BANKS = 8
 EARLY = 8
 HALF = T // 2
 LAG = 3
+WARM = 30
 VECTOR_COLS = 160
 
 
@@ -44,9 +45,11 @@ def tile_mix_xres_fm_silu_kernel(tc, x4_words, x4_scales, xr, w4_words, w4_scale
         wl_scales = keep.tile([P, PASSES, (TILES - EARLY) * P], U8, align_bytes=256)
         warm = keep.tile([P, 1], F32)
         warm_out = keep.tile([P, 1], F32)
+        zeros = keep.tile([P, P], F32)
         b_rows = keep.tile([P, 32], F32, align_bytes=64)
         b_cols = keep.tile([P, 32], F32, align_bytes=64)
 
+        nc.gpsimd.memset(zeros[:], 0.0)
         nc.vector.memset(x_scales[:].bitcast(I32), 0)
         nc.vector.memset(we_scales[:].bitcast(I32), 0)
         nc.vector.memset(b_rows[:], 0.0)
@@ -121,41 +124,62 @@ def tile_mix_xres_fm_silu_kernel(tc, x4_words, x4_scales, xr, w4_words, w4_scale
         banks = {}
         done = {}
 
+        def stationary(i, a):
+            if i < EARLY:
+                g, k = divmod(i, half_early)
+                return (
+                    we_words[a][g][:, 2 * P * k : 2 * P * (k + 1)].bitcast(FP4X4),
+                    we_scales[:, a, P * i : P * (i + 1)],
+                )
+            k = i - EARLY
+            return (
+                wl_words[:, a, 2 * P * k : 2 * P * (k + 1)].bitcast(FP4X4),
+                wl_scales[:, a, P * k : P * (k + 1)],
+            )
+
+        def moving(kind, a, t0, t1):
+            if kind == "x4":
+                return x_words[a][:, 2 * t0 : 2 * t1].bitcast(FP4X4), x_scales[:, a, t0:t1]
+            return codes[a][:, t0:t1].bitcast(FP8X4), scales[a][:, t0:t1]
+
+        def multiply(acc, kind, i, a, t0, t1, start, stop):
+            w_view, w_scale = stationary(i, a)
+            x_view, x_scale = moving(kind, a, t0, t1)
+            nc.tensor.matmul_mx(
+                out=acc, lhsT=w_view, lhsT_scale=w_scale, rhs=x_view, rhs_scale=x_scale, start=start, stop=stop
+            )
+
         def mx_pass(kind, i, a):
             if i not in banks:
                 banks[i] = psum.tile([P, T], F32, name="acc%d" % i, tag="bank%d" % (i % BANKS))
                 done[i] = 0
-            if i < EARLY:
-                g, k = divmod(i, half_early)
-                lhsT = we_words[a][g][:, 2 * P * k : 2 * P * (k + 1)].bitcast(FP4X4)
-                lhsT_scale = we_scales[:, a, P * i : P * (i + 1)]
-            else:
-                j = i - EARLY
-                lhsT = wl_words[:, a, 2 * P * j : 2 * P * (j + 1)].bitcast(FP4X4)
-                lhsT_scale = wl_scales[:, a, P * j : P * (j + 1)]
-            if kind == "x4":
-                rhs = x_words[a][:].bitcast(FP4X4)
-                rhs_scale = x_scales[:, a, :]
-            else:
-                rhs = codes[a][:].bitcast(FP8X4)
-                rhs_scale = scales[a][:]
-            nc.tensor.matmul_mx(
-                out=banks[i][:], lhsT=lhsT, lhsT_scale=lhsT_scale, rhs=rhs, rhs_scale=rhs_scale,
-                start=done[i] == 0, stop=done[i] == 3,
-            )
+            multiply(banks[i][:], kind, i, a, 0, T, done[i] == 0, done[i] == 3)
             done[i] += 1
             if done[i] == 4:
-                finish(i)
+                res = keep.tile([P, T], F32, name="res%d" % i)
+                nc.scalar.activation(res[:], banks[i][:], SILU, bias=b_cols[:, i : i + 1])
+                nc.sync.dma_start(out=out[P * i : P * (i + 1), :], in_=res[:])
 
-        def finish(i):
-            pieces = 2 if i == TILES - 1 else 1
-            width = T // pieces
-            for c in range(pieces):
-                cols = slice(c * width, (c + 1) * width)
-                res = keep.tile([P, width], F32, name="res%d_%d" % (i, c))
-                nc.scalar.activation(res[:], banks[i][:, cols], SILU, bias=b_cols[:, i : i + 1])
-                nc.sync.dma_start(out=out[P * i : P * (i + 1), cols], in_=res[:])
+        def last_tile(i):
+            res = keep.tile([P, T], F32, name="res_last")
+            for n in range(4):
+                t0, t1 = n * P, (n + 1) * P
+                acc = psum.tile([P, P], F32, name="acc_last%d" % n, tag="bank%d" % (3 + n))
+                multiply(acc[:], "x4", i, 0, t0, t1, True, False)
+                multiply(acc[:], "x4", i, 1, t0, t1, False, False)
+                multiply(acc[:], "xr", i, 0, t0, t1, False, False)
+                multiply(acc[:], "xr", i, 1, t0, t1, False, True)
+                nc.scalar.activation(res[:, t0:t1], acc[:], SILU, bias=b_cols[:, i : i + 1])
+                if n == 1:
+                    nc.sync.dma_start(out=out[P * i : P * (i + 1), 0:t1], in_=res[:, 0:t1])
+                if n == 2:
+                    nc.sync.dma_start(out=out[P * i : P * (i + 1), t0:t1], in_=res[:, t0:t1])
+                if n == 3:
+                    nc.scalar.dma_start(out=out[P * i : P * (i + 1), t0:t1], in_=res[:, t0:t1])
 
+        idle = psum.tile([P, P], F32, tag="bank%d" % (BANKS - 1), name="idle")
+        for n in range(WARM):
+            nc.tensor.transpose(idle[:], zeros[:], zeros[:])
         for a in range(PASSES):
             for i in range(BANKS):
                 mx_pass("x4", i, a)
@@ -165,7 +189,8 @@ def tile_mix_xres_fm_silu_kernel(tc, x4_words, x4_scales, xr, w4_words, w4_scale
             mx_pass("xr", i, 1)
             if i + LAG < BANKS:
                 mx_pass("xr", i + LAG, 0)
-        for i in range(BANKS, TILES):
+        for i in range(BANKS, TILES - 1):
             for kind in ("x4", "xr"):
                 for a in range(PASSES):
                     mx_pass(kind, i, a)
+        last_tile(TILES - 1)

from contextlib import ExitStack

import concourse.mybir as mybir

K, M, T = 1024, 1536, 512
FLOPS = 2 * 2 * K * M * T

F32 = mybir.dt.float32
BF16 = mybir.dt.bfloat16
I32 = mybir.dt.int32
U32 = mybir.dt.uint32
U8 = mybir.dt.uint8
FP8X4 = mybir.dt.float8_e4m3fn_x4
FP4X4 = mybir.dt.float4_e2m1fn_x4
SILU = mybir.ActivationFunctionType.Silu

P = 128
PACK = 4
PASSES = 2
TILES = M // P
BANKS = 8
EARLY = 8
HALF = T // 2
LAG = 3
WARM = 30
VECTOR_COLS = 160


def tile_mix_xres_fm_silu_kernel(tc, x4_words, x4_scales, xr, w4_words, w4_scales, b, out):
    nc = tc.nc
    with ExitStack() as ctx:
        keep = ctx.enter_context(tc.tile_pool(name="keep", bufs=1))
        psum = ctx.enter_context(tc.psum_pool(name="psum", bufs=1))
        ctx.enter_context(tc.manual_schedule())

        x_words = [keep.tile([P, 2 * T], U8, align_bytes=256, name="x_words%d" % a) for a in range(PASSES)]
        x_scales = keep.tile([P, PASSES, T], U8, align_bytes=256)
        half_early = EARLY // 2
        we_words = [
            [keep.tile([P, half_early * 2 * P], U8, align_bytes=256, name="we_words%d_%d" % (a, g)) for g in range(2)]
            for a in range(PASSES)
        ]
        we_scales = keep.tile([P, PASSES, EARLY * P], U8, align_bytes=256)
        wl_words = keep.tile([P, PASSES, (TILES - EARLY) * 2 * P], U8, align_bytes=256)
        wl_scales = keep.tile([P, PASSES, (TILES - EARLY) * P], U8, align_bytes=256)
        warm = keep.tile([P, 1], F32)
        warm_out = keep.tile([P, 1], F32)
        zeros = keep.tile([P, P], F32)
        b_rows = keep.tile([P, 32], F32, align_bytes=64)
        b_cols = keep.tile([P, 32], F32, align_bytes=64)

        nc.gpsimd.memset(zeros[:], 0.0)
        nc.vector.memset(x_scales[:].bitcast(I32), 0)
        nc.vector.memset(we_scales[:].bitcast(I32), 0)
        nc.vector.memset(b_rows[:], 0.0)
        nc.vector.memset(warm[:], 0.0)
        nc.vector.memset(wl_scales[:].bitcast(I32), 0)

        xw = x4_words.bitcast(I32).rearrange("a p n -> p a n")
        ww = w4_words.bitcast(I32)
        xs = x4_scales.bitcast(I32).rearrange("a (q r) n -> r q a n", r=4)
        ws = w4_scales.bitcast(I32).rearrange("a (q r) n -> r q a n", r=4)
        e_words = EARLY * 2 * P // 4
        e_scales = EARLY * P // 4

        nc.sync.dma_start(out=x_words[0][:].bitcast(I32), in_=xw[:, 0])
        nc.scalar.dma_start(out=we_words[0][0][:].bitcast(I32), in_=ww[0, :, 0 : e_words // 2])
        b_view = b.rearrange("(i q c) -> q i c", q=4, c=32)
        for q in range(4):
            nc.gpsimd.dma_start(out=b_rows[32 * q : 32 * q + TILES, :], in_=b_view[q])

        for r in range(4):
            nc.sync.dma_start(out=x_scales[:].bitcast(I32)[r:P:32], in_=xs[r])
        for r in range(4):
            queue = nc.scalar if r < 2 else nc.sync
            queue.dma_start(out=we_scales[:].bitcast(I32)[r:P:32], in_=ws[r, :, :, 0:e_scales])
        nc.sync.dma_start(out=we_words[0][1][:].bitcast(I32), in_=ww[0, :, e_words // 2 : e_words])
        nc.sync.dma_start(out=x_words[1][:].bitcast(I32), in_=xw[:, 1])
        for g in range(2):
            nc.sync.dma_start(
                out=we_words[1][g][:].bitcast(I32), in_=ww[1, :, g * e_words // 2 : (g + 1) * e_words // 2]
            )
        nc.scalar.activation(warm_out[:], warm[:], SILU)

        xr_view = xr.rearrange("(a p j) t -> a p j t", p=P, j=PACK)
        raw = [keep.tile([P, PACK, T], F32, name="raw%d" % a) for a in range(PASSES)]
        nc.sync.dma_start(out=raw[0][:], in_=xr_view[0])
        for h in range(2):
            cols = slice(h * HALF, (h + 1) * HALF)
            nc.sync.dma_start(out=raw[1][:, :, cols], in_=xr_view[1, :, :, cols])
        nc.sync.dma_start(out=wl_words[:].bitcast(I32), in_=ww.rearrange("a p n -> p a n")[:, :, e_words:])
        for r in range(4):
            nc.sync.dma_start(out=wl_scales[:].bitcast(I32)[r:P:32], in_=ws[r, :, :, e_scales:])

        grouped = [keep.tile([P, T, PACK], BF16, align_bytes=256, name="grouped%d" % a) for a in range(PASSES)]
        codes = [keep.tile([P, T], U32, align_bytes=256, name="codes%d" % a) for a in range(PASSES)]
        scales = [keep.tile([P, T], U8, align_bytes=256, name="scales%d" % a) for a in range(PASSES)]

        def interleave(a, h):
            c0 = h * HALF
            c1 = c0 + VECTOR_COLS
            c2 = c0 + HALF
            nc.vector.tensor_copy(out=grouped[a][:, c0:c1, :], in_=raw[a][:, :, c0:c1].rearrange("p j t -> p t j"))
            nc.scalar.copy(out=grouped[a][:, c1:c2, :], in_=raw[a][:, :, c1:c2].rearrange("p j t -> p t j"))

        def quantize(a, h):
            cols = slice(h * HALF, (h + 1) * HALF)
            nc.vector.quantize_mx(
                out=codes[a][:, cols].bitcast(FP8X4),
                scales=scales[a][:, cols],
                in_=grouped[a][:, cols, :].rearrange("p t j -> p (t j)"),
            )

        interleave(0, 0)
        interleave(0, 1)
        quantize(0, 0)
        quantize(0, 1)
        interleave(1, 0)
        quantize(1, 0)
        interleave(1, 1)
        quantize(1, 1)
        nc.vector.transpose(b_cols[:], b_rows[:])

        banks = {}
        done = {}

        def stationary(i, a):
            if i < EARLY:
                g, k = divmod(i, half_early)
                return (
                    we_words[a][g][:, 2 * P * k : 2 * P * (k + 1)].bitcast(FP4X4),
                    we_scales[:, a, P * i : P * (i + 1)],
                )
            k = i - EARLY
            return (
                wl_words[:, a, 2 * P * k : 2 * P * (k + 1)].bitcast(FP4X4),
                wl_scales[:, a, P * k : P * (k + 1)],
            )

        def moving(kind, a, t0, t1):
            if kind == "x4":
                return x_words[a][:, 2 * t0 : 2 * t1].bitcast(FP4X4), x_scales[:, a, t0:t1]
            return codes[a][:, t0:t1].bitcast(FP8X4), scales[a][:, t0:t1]

        def multiply(acc, kind, i, a, t0, t1, start, stop):
            w_view, w_scale = stationary(i, a)
            x_view, x_scale = moving(kind, a, t0, t1)
            nc.tensor.matmul_mx(
                out=acc, lhsT=w_view, lhsT_scale=w_scale, rhs=x_view, rhs_scale=x_scale, start=start, stop=stop
            )

        def mx_pass(kind, i, a):
            if i not in banks:
                banks[i] = psum.tile([P, T], F32, name="acc%d" % i, tag="bank%d" % (i % BANKS))
                done[i] = 0
            multiply(banks[i][:], kind, i, a, 0, T, done[i] == 0, done[i] == 3)
            done[i] += 1
            if done[i] == 4:
                res = keep.tile([P, T], F32, name="res%d" % i)
                nc.scalar.activation(res[:], banks[i][:], SILU, bias=b_cols[:, i : i + 1])
                nc.sync.dma_start(out=out[P * i : P * (i + 1), :], in_=res[:])

        def last_tile(i):
            res = keep.tile([P, T], F32, name="res_last")
            for n in range(4):
                t0, t1 = n * P, (n + 1) * P
                acc = psum.tile([P, P], F32, name="acc_last%d" % n, tag="bank%d" % (3 + n))
                multiply(acc[:], "x4", i, 0, t0, t1, True, False)
                multiply(acc[:], "x4", i, 1, t0, t1, False, False)
                multiply(acc[:], "xr", i, 0, t0, t1, False, False)
                multiply(acc[:], "xr", i, 1, t0, t1, False, True)
                nc.scalar.activation(res[:, t0:t1], acc[:], SILU, bias=b_cols[:, i : i + 1])
                if n == 1:
                    nc.sync.dma_start(out=out[P * i : P * (i + 1), 0:t1], in_=res[:, 0:t1])
                if n == 2:
                    nc.sync.dma_start(out=out[P * i : P * (i + 1), t0:t1], in_=res[:, t0:t1])
                if n == 3:
                    nc.scalar.dma_start(out=out[P * i : P * (i + 1), t0:t1], in_=res[:, t0:t1])

        idle = psum.tile([P, P], F32, tag="bank%d" % (BANKS - 1), name="idle")
        for n in range(WARM):
            nc.tensor.transpose(idle[:], zeros[:], zeros[:])
        for a in range(PASSES):
            for i in range(BANKS):
                mx_pass("x4", i, a)
        for i in range(LAG):
            mx_pass("xr", i, 0)
        for i in range(BANKS):
            mx_pass("xr", i, 1)
            if i + LAG < BANKS:
                mx_pass("xr", i + LAG, 0)
        for i in range(BANKS, TILES - 1):
            for kind in ("x4", "xr"):
                for a in range(PASSES):
                    mx_pass(kind, i, a)
        last_tile(TILES - 1)
